import numpy as np
CORES = [6,14,22,30,134,142,150,158,262,270,278,286,390,398,406,414]
N = 16
T = 128
ROUTE = [[[11],[2],[10],[5],[1],[1],[15],[13],[14],[8],[0],[1],[8],[5],[9],[0],[2],[14],[12],[14],[7],[2],[2],[13],[0],[6],[1],[14],[15],[11],[4],[4],[13],[8],[2],[0],[2],[10],[3],[10],[11],[13],[15],[8],[7],[9],[10],[14],[6],[5],[9],[12],[8],[3],[4],[8],[2],[8],[2],[15],[11],[2],[14],[2],[13],[3],[11],[12],[7],[4],[12],[1],[3],[14],[0],[7],[1],[0],[4],[5],[10],[0],[15],[1],[1],[2],[8],[4],[6],[5],[5],[4],[14],[14],[9],[13],[7],[2],[6],[14],[11],[9],[4],[7],[6],[8],[4],[8],[7],[1],[11],[1],[1],[1],[3],[3],[15],[12],[13],[7],[0],[15],[5],[9],[8],[13],[12],[2]],[[11],[2],[9],[5],[15],[10],[5],[1],[15],[1],[6],[14],[4],[13],[5],[1],[11],[2],[8],[14],[4],[13],[9],[12],[14],[7],[4],[10],[0],[10],[2],[12],[5],[15],[6],[8],[6],[3],[9],[2],[12],[12],[8],[1],[5],[5],[7],[9],[12],[8],[13],[6],[15],[8],[11],[4],[10],[4],[2],[11],[13],[9],[10],[13],[7],[12],[14],[10],[2],[6],[5],[1],[0],[6],[7],[0],[3],[10],[10],[4],[6],[10],[14],[10],[7],[5],[13],[7],[0],[2],[13],[13],[10],[1],[13],[7],[15],[7],[8],[7],[8],[11],[6],[11],[15],[10],[7],[9],[5],[5],[14],[15],[2],[5],[15],[3],[9],[11],[12],[2],[0],[14],[1],[11],[13],[8],[5],[13]],[[3],[7],[10],[8],[14],[8],[0],[5],[1],[9],[1],[0],[0],[6],[10],[10],[5],[10],[0],[14],[10],[7],[11],[8],[4],[10],[9],[2],[4],[13],[6],[0],[6],[10],[15],[4],[9],[10],[6],[13],[2],[1],[14],[10],[3],[3],[14],[2],[8],[10],[3],[2],[12],[15],[9],[7],[11],[4],[10],[7],[14],[1],[15],[14],[14],[15],[8],[14],[15],[6],[15],[9],[15],[0],[1],[11],[13],[9],[14],[10],[10],[5],[11],[8],[15],[15],[1],[2],[9],[10],[10],[2],[9],[1],[12],[3],[2],[6],[10],[10],[1],[4],[11],[6],[1],[11],[10],[12],[10],[4],[10],[8],[4],[8],[5],[15],[12],[6],[0],[5],[6],[1],[5],[12],[0],[11],[2],[3]],[[9],[11],[13],[15],[13],[9],[12],[9],[0],[15],[12],[0],[4],[12],[13],[4],[12],[2],[15],[1],[13],[15],[6],[11],[9],[13],[0],[10],[7],[9],[10],[6],[15],[0],[15],[6],[5],[13],[6],[11],[3],[5],[15],[13],[6],[1],[13],[7],[6],[11],[8],[13],[12],[13],[6],[11],[0],[7],[6],[1],[13],[7],[11],[11],[11],[2],[0],[15],[4],[8],[7],[4],[5],[9],[10],[1],[6],[6],[8],[6],[8],[7],[13],[8],[15],[2],[2],[10],[0],[2],[9],[0],[0],[13],[14],[0],[8],[13],[8],[7],[13],[1],[14],[6],[7],[13],[9],[7],[7],[8],[5],[7],[0],[11],[9],[7],[0],[9],[10],[0],[11],[13],[8],[1],[14],[14],[15],[6]],[[8],[1],[4],[5],[5],[14],[7],[1],[14],[9],[8],[9],[7],[13],[15],[10],[8],[7],[15],[14],[8],[12],[14],[1],[2],[2],[12],[7],[1],[9],[0],[7],[15],[4],[5],[15],[7],[11],[9],[1],[4],[14],[4],[5],[0],[5],[14],[1],[8],[12],[10],[11],[12],[14],[8],[11],[14],[14],[8],[9],[7],[2],[13],[8],[0],[13],[11],[0],[2],[9],[14],[9],[14],[8],[1],[7],[8],[14],[5],[10],[14],[5],[1],[0],[2],[1],[11],[7],[0],[3],[3],[6],[5],[9],[4],[1],[15],[10],[6],[7],[2],[12],[3],[10],[12],[14],[4],[0],[6],[12],[0],[2],[7],[5],[3],[8],[1],[7],[13],[7],[4],[12],[15],[4],[15],[12],[1],[7]],[[9],[3],[12],[4],[5],[10],[2],[13],[11],[7],[6],[4],[14],[5],[5],[0],[5],[11],[2],[6],[14],[6],[1],[8],[1],[2],[10],[8],[15],[6],[11],[5],[12],[13],[4],[5],[5],[1],[15],[8],[6],[8],[8],[1],[7],[8],[1],[8],[12],[6],[0],[3],[5],[3],[4],[12],[13],[13],[8],[14],[6],[14],[9],[12],[6],[15],[0],[4],[13],[12],[4],[5],[9],[1],[12],[14],[10],[15],[14],[1],[6],[13],[9],[12],[10],[14],[9],[1],[13],[13],[7],[5],[14],[10],[14],[9],[13],[10],[3],[8],[4],[5],[14],[4],[15],[3],[4],[11],[10],[15],[6],[14],[12],[10],[7],[4],[10],[9],[4],[12],[11],[3],[1],[12],[15],[9],[3],[10]],[[2],[7],[7],[13],[10],[9],[15],[9],[14],[8],[1],[14],[9],[6],[11],[1],[12],[5],[12],[0],[9],[7],[4],[15],[5],[11],[11],[10],[1],[14],[12],[15],[11],[6],[7],[4],[3],[5],[4],[7],[1],[2],[12],[4],[10],[11],[5],[4],[0],[15],[0],[15],[7],[13],[14],[14],[8],[9],[7],[11],[0],[6],[6],[14],[2],[10],[2],[0],[4],[7],[5],[6],[3],[8],[13],[9],[1],[9],[8],[14],[12],[9],[12],[10],[3],[14],[6],[6],[2],[11],[5],[1],[4],[2],[10],[8],[7],[13],[7],[1],[2],[13],[0],[7],[2],[3],[6],[6],[6],[0],[3],[8],[12],[0],[5],[0],[2],[12],[7],[2],[4],[5],[15],[5],[0],[7],[11],[15]],[[10],[9],[6],[3],[6],[15],[11],[0],[1],[13],[15],[9],[2],[9],[15],[5],[10],[5],[10],[1],[5],[9],[1],[12],[9],[7],[10],[10],[5],[13],[15],[0],[1],[13],[3],[4],[9],[0],[6],[8],[13],[8],[3],[5],[5],[3],[9],[8],[2],[0],[14],[2],[10],[14],[5],[0],[11],[7],[4],[2],[14],[9],[15],[7],[4],[0],[9],[8],[2],[1],[8],[9],[4],[12],[0],[5],[6],[5],[11],[1],[10],[6],[4],[3],[5],[8],[5],[11],[0],[8],[1],[10],[5],[3],[8],[14],[12],[5],[15],[4],[2],[15],[1],[4],[6],[12],[10],[4],[11],[15],[2],[10],[12],[15],[10],[14],[8],[12],[10],[12],[9],[9],[5],[14],[5],[11],[11],[9]],[[11],[1],[1],[6],[9],[13],[14],[9],[9],[2],[14],[15],[4],[8],[6],[10],[12],[15],[8],[10],[2],[13],[14],[0],[12],[2],[14],[6],[11],[12],[8],[13],[1],[14],[12],[11],[15],[6],[7],[11],[10],[11],[3],[10],[2],[12],[1],[14],[12],[14],[15],[9],[7],[5],[10],[4],[15],[12],[3],[11],[3],[5],[11],[10],[4],[4],[8],[3],[8],[10],[0],[1],[7],[14],[5],[9],[3],[8],[6],[3],[7],[5],[10],[13],[9],[15],[13],[5],[8],[14],[14],[2],[3],[1],[3],[8],[6],[8],[15],[7],[10],[14],[7],[8],[5],[1],[8],[3],[4],[1],[13],[15],[1],[9],[6],[1],[4],[10],[6],[11],[3],[12],[15],[6],[14],[15],[3],[8]],[[10],[8],[9],[7],[0],[13],[12],[12],[14],[0],[14],[2],[11],[0],[13],[6],[10],[1],[5],[15],[0],[3],[13],[11],[0],[14],[12],[4],[10],[0],[5],[14],[15],[13],[12],[12],[6],[13],[13],[0],[3],[15],[5],[6],[4],[12],[2],[8],[11],[1],[5],[9],[6],[10],[7],[0],[10],[1],[8],[7],[9],[15],[2],[3],[14],[2],[11],[6],[15],[7],[9],[2],[0],[1],[9],[11],[11],[3],[1],[2],[4],[10],[15],[6],[8],[14],[8],[5],[14],[5],[6],[2],[15],[13],[14],[5],[6],[2],[3],[15],[11],[15],[8],[3],[2],[7],[11],[5],[7],[8],[4],[9],[5],[6],[7],[6],[2],[12],[2],[9],[13],[6],[2],[1],[14],[9],[14],[11]],[[7],[5],[9],[15],[9],[12],[14],[8],[8],[14],[15],[15],[6],[13],[10],[12],[12],[12],[15],[1],[1],[9],[6],[14],[9],[6],[13],[12],[2],[15],[14],[2],[9],[6],[11],[13],[10],[2],[0],[13],[6],[2],[11],[3],[2],[13],[5],[13],[8],[13],[0],[11],[3],[0],[5],[15],[2],[9],[4],[13],[15],[15],[2],[15],[4],[10],[11],[13],[7],[8],[2],[12],[9],[15],[4],[5],[2],[0],[3],[9],[12],[13],[10],[10],[13],[0],[2],[10],[9],[13],[11],[10],[0],[12],[10],[3],[1],[5],[14],[4],[11],[11],[3],[11],[12],[9],[2],[3],[14],[15],[11],[14],[4],[2],[1],[12],[6],[7],[0],[13],[7],[4],[10],[7],[15],[6],[1],[12]],[[2],[7],[11],[13],[3],[8],[5],[0],[4],[12],[8],[5],[9],[0],[12],[13],[13],[7],[6],[8],[13],[3],[0],[8],[4],[8],[5],[11],[7],[8],[1],[13],[14],[8],[11],[9],[0],[4],[5],[15],[1],[7],[3],[15],[0],[9],[9],[14],[6],[13],[14],[0],[10],[6],[0],[8],[15],[4],[11],[13],[15],[14],[9],[12],[2],[2],[2],[1],[9],[3],[14],[5],[7],[14],[14],[13],[14],[5],[13],[4],[14],[3],[2],[4],[12],[14],[11],[0],[12],[4],[14],[14],[12],[13],[2],[6],[15],[5],[2],[13],[6],[3],[4],[10],[9],[1],[12],[9],[6],[14],[9],[4],[6],[0],[9],[0],[15],[13],[11],[2],[14],[12],[7],[7],[3],[10],[8],[14]],[[8],[8],[10],[6],[1],[15],[15],[0],[14],[7],[6],[0],[14],[13],[13],[12],[3],[1],[13],[9],[15],[7],[9],[8],[4],[6],[2],[15],[4],[11],[4],[8],[4],[11],[6],[10],[1],[2],[8],[12],[13],[11],[7],[10],[0],[10],[3],[15],[4],[2],[7],[3],[11],[12],[0],[2],[4],[0],[15],[11],[1],[5],[14],[6],[3],[8],[1],[0],[2],[1],[3],[7],[3],[14],[13],[0],[13],[5],[7],[14],[10],[5],[13],[7],[2],[7],[11],[15],[0],[12],[7],[10],[3],[13],[3],[10],[3],[2],[13],[12],[2],[5],[10],[6],[9],[12],[10],[14],[12],[12],[7],[3],[3],[6],[12],[11],[15],[4],[10],[5],[14],[8],[11],[12],[9],[0],[9],[1]],[[1],[14],[5],[15],[4],[6],[12],[10],[5],[10],[4],[8],[6],[8],[14],[9],[12],[6],[2],[8],[14],[10],[7],[1],[14],[13],[5],[2],[10],[8],[10],[12],[11],[10],[15],[14],[13],[2],[5],[8],[6],[13],[10],[9],[10],[0],[12],[9],[2],[2],[0],[2],[4],[2],[4],[10],[14],[7],[11],[5],[0],[13],[3],[13],[0],[7],[3],[6],[13],[9],[0],[2],[11],[11],[4],[5],[3],[8],[1],[12],[3],[6],[2],[15],[14],[9],[13],[15],[11],[10],[10],[8],[0],[7],[11],[14],[0],[0],[6],[9],[15],[2],[8],[7],[5],[2],[0],[5],[10],[1],[14],[4],[4],[5],[13],[10],[5],[1],[10],[1],[0],[6],[4],[2],[9],[2],[12],[5]],[[12],[5],[8],[9],[0],[12],[7],[12],[11],[8],[3],[8],[6],[0],[0],[7],[6],[3],[4],[13],[4],[5],[2],[8],[10],[7],[10],[9],[1],[1],[9],[7],[1],[2],[3],[9],[14],[1],[14],[2],[5],[13],[3],[15],[2],[8],[11],[13],[10],[6],[15],[4],[4],[15],[10],[1],[7],[4],[0],[15],[10],[15],[12],[2],[14],[11],[5],[5],[0],[0],[7],[10],[1],[7],[3],[11],[4],[2],[10],[4],[5],[0],[3],[9],[4],[15],[15],[2],[3],[14],[0],[2],[14],[11],[3],[13],[1],[3],[1],[5],[1],[5],[2],[4],[9],[12],[8],[0],[1],[12],[2],[11],[13],[0],[7],[6],[13],[10],[0],[12],[7],[14],[9],[10],[3],[10],[15],[3]],[[10],[3],[10],[10],[11],[8],[13],[9],[14],[3],[6],[5],[4],[7],[0],[8],[3],[13],[9],[14],[15],[4],[0],[2],[10],[15],[13],[4],[5],[14],[7],[15],[11],[5],[1],[6],[3],[8],[9],[3],[5],[13],[6],[5],[0],[15],[2],[0],[15],[8],[9],[0],[0],[10],[15],[0],[7],[4],[12],[8],[13],[11],[13],[12],[12],[15],[5],[0],[4],[5],[7],[9],[7],[14],[13],[12],[4],[2],[10],[3],[15],[0],[6],[9],[0],[3],[7],[4],[2],[8],[5],[11],[11],[9],[3],[15],[7],[8],[2],[10],[7],[2],[8],[0],[2],[12],[0],[15],[6],[12],[10],[8],[14],[13],[4],[5],[10],[8],[12],[9],[10],[15],[8],[4],[12],[7],[14],[11]]]
YW = 147
def setup_inputs(rng):
    return {"x": rng.standard_normal((N, 128, T), dtype=np.float32)}
def reference(x):
    y = np.full((N, 128, YW), np.nan, x.dtype)
    fill = [0] * N
    for r in range(N):
        for t in range(T):
            for e in ROUTE[r][t]:
                y[e][:, fill[e]] = x[r][:, t]
                fill[e] += 1
    return {"y": y}

@@ -1,0 +1,140 @@
+from concourse.bass import DstId, RemoteDMATransfer
+
+SCRATCH = {
+    "xs": ("sbuf", [128, 128], "float32"),
+    "land": ("sbuf", [128, 147], "float32"),
+}
+SEMAPHORES = ["loaded", "rep", "arr", "sent", "stored"]
+
+PLAN = {}
+
+
+def match(elig, cap):
+    owner = {}
+
+    def place(t, seen):
+        for n in elig[t]:
+            if n in seen:
+                continue
+            seen.add(n)
+            lst = owner.setdefault(n, [])
+            if len(lst) < cap:
+                lst.append(t)
+                return True
+            for j in range(len(lst)):
+                if place(lst[j], seen):
+                    lst[j] = t
+                    return True
+        return False
+
+    for t in range(len(elig)):
+        if not place(t, set()):
+            return None
+    return owner
+
+
+def masks(n, base):
+    k = 8
+    while k * n > 8:
+        k //= 2
+    return [((1 << k) - 1) << (base + i * k) for i in range(n)]
+
+
+def build_plan(cores, route, topo):
+    n = len(cores)
+    ntok = len(route[0])
+    fill = [0] * n
+    pos = []
+    for r in range(n):
+        row = []
+        for t in range(ntok):
+            e = route[r][t][0]
+            row.append(fill[e])
+            fill[e] += 1
+        pos.append(row)
+    plan = {"count": fill, "rep": {}, "wait": {}, "calls": {}, "arr": [0] * n}
+    for r in range(n):
+        me = cores[r]
+        h, c = topo.host(me), topo.chip(me)
+        base = me - me % 8
+        team = [(base + k, i) for i, k in enumerate((0, 1, 4, 5))]
+        team += [(base + k, i) for i, k in enumerate((2, 3, 7))]
+        for m in (1, 2):
+            team += [((h ^ 1) * 128 + (c + 4 * m) * 8 + k, i) for i, k in enumerate((2, 3, 6, 7))]
+        owner = None
+        w = 28
+        while owner is None:
+            w += 4
+            start = [max(0, min(ntok - w, 32 * i - (w - 32) // 2)) for i in range(4)]
+            hold = [(k, start[i], start[i] + w) for k, i in team] + [(me, 0, ntok)]
+            elig = []
+            for t in range(ntok):
+                d = cores[route[r][t][0]]
+                el = []
+                for i, (k, s, e) in enumerate(hold):
+                    if k != d and s <= t < e and topo.may_write(k, d):
+                        el.append(2 * i + (1 if k // 8 == d // 8 else 0))
+                elig.append(el)
+            owner = match(elig, 8)
+        busy = set()
+        for i, (k, s, e) in enumerate(hold):
+            call = []
+            for on in (0, 1):
+                toks = sorted(owner.get(2 * i + on, []))
+                for t, mk in zip(toks, masks(len(toks), 8 * on)):
+                    x = route[r][t][0]
+                    call.append((t, cores[x], pos[r][t], mk))
+                    plan["arr"][x] += bin(mk).count("1")
+            if call:
+                plan["calls"][k] = [call]
+                busy.add(k)
+        rep = []
+        for i in range(4):
+            for on in (0, 1):
+                dsts = [k for k, j in team if j == i and k in busy and (k // 8 == me // 8) == (on == 1)]
+                if dsts:
+                    rep.append((start[i], w, dsts, 3 << (8 * on + 2 * i)))
+                    for k in dsts:
+                        plan["wait"][k] = 2
+        plan["rep"][me] = rep
+    return plan
+
+
+def rank_program(g, core, T, topo):
+    if "p" not in PLAN:
+        PLAN["p"] = build_plan(T.cores, T.tables["ROUTE"], topo)
+    p = PLAN["p"]
+    rank = T.rank_of(core)
+    if rank is None and core not in p["wait"]:
+        return
+    sem = T.sem
+
+    def dst_id(d):
+        rid, pid = topo.addr(d, core)
+        return DstId(rid=rid, pnc=pid)
+
+    sent = 0
+    if rank is not None:
+        g.sync.dma_start(T.xs[:, :], T.x[:, :]).then_inc(sem.loaded, 16)
+        g.wait_ge(sem.loaded, 16)
+        trs = []
+        for s, w, dsts, mk in p["rep"][core]:
+            trs.append(RemoteDMATransfer(dst_ids=[dst_id(d) for d in dsts], dma_engine_mask=mk, remote_sem=sem.rep,
+                                         srcs=[T.xs[:, s:s + w]], dsts=[T.xs[:, s:s + w] for d in dsts]))
+            sent += bin(mk).count("1")
+        g.remote_dma_fused(trs, local_sem=sem.sent)
+    else:
+        g.wait_ge(sem.rep, p["wait"][core])
+    for call in p["calls"].get(core, []):
+        trs = []
+        for t, d, j, mk in call:
+            trs.append(RemoteDMATransfer(dst_ids=[dst_id(d)], dma_engine_mask=mk, remote_sem=sem.arr,
+                                         src=T.xs[:, t:t + 1], dst=T.land[:, j:j + 1]))
+            sent += bin(mk).count("1")
+        g.remote_dma_fused(trs, local_sem=sem.sent)
+    if rank is not None:
+        cnt = p["count"][rank]
+        g.sync.wait_ge(sem.arr, p["arr"][rank])
+        g.sync.dma_start(T.y[:, 0:cnt], T.land[:, 0:cnt]).then_inc(sem.stored, 16)
+        g.wait_ge(sem.stored, 16)
+    g.wait_ge(sem.sent, sent)

@@ -7,6 +7,8 @@ SCRATCH = {
 SEMAPHORES = ["loaded", "rep", "arr", "sent", "stored"]
 
 PLAN = {}
+CAPS = (12, 10, 6, 5)
+RANK_CAP = 4
 
 
 def match(elig, cap):
@@ -18,7 +20,7 @@ def match(elig, cap):
                 continue
             seen.add(n)
             lst = owner.setdefault(n, [])
-            if len(lst) < cap:
+            if len(lst) < cap[n]:
                 lst.append(t)
                 return True
             for j in range(len(lst)):
@@ -40,6 +42,16 @@ def masks(n, base):
     return [((1 << k) - 1) << (base + i * k) for i in range(n)]
 
 
+def chunks(toks):
+    out = []
+    i = 0
+    for size in (8, 8, 4, 2, 1):
+        if len(toks) - i >= size:
+            out.append(toks[i:i + size])
+            i += size
+    return out
+
+
 def build_plan(cores, route, topo):
     n = len(cores)
     ntok = len(route[0])
@@ -53,50 +65,67 @@ def build_plan(cores, route, topo):
             fill[e] += 1
         pos.append(row)
     plan = {"count": fill, "rep": {}, "wait": {}, "calls": {}, "arr": [0] * n}
+    tot = sum(CAPS)
+    edge = [0]
+    for x in CAPS:
+        edge.append(edge[-1] + ntok * x / tot)
     for r in range(n):
         me = cores[r]
         h, c = topo.host(me), topo.chip(me)
         base = me - me % 8
-        team = [(base + k, i) for i, k in enumerate((0, 1, 4, 5))]
-        team += [(base + k, i) for i, k in enumerate((2, 3, 7))]
-        for m in (1, 2):
-            team += [((h ^ 1) * 128 + (c + 4 * m) * 8 + k, i) for i, k in enumerate((2, 3, 6, 7))]
+        far = (h ^ 1) * 128 + c * 8
         owner = None
-        w = 28
+        m = -1
         while owner is None:
-            w += 4
-            start = [max(0, min(ntok - w, 32 * i - (w - 32) // 2)) for i in range(4)]
-            hold = [(k, start[i], start[i] + w) for k, i in team] + [(me, 0, ntok)]
+            m += 1
+            hold = []
+            for i, x in enumerate(CAPS):
+                w = min(ntok, -(-ntok * x // tot) + 2 * m)
+                mid = (edge[i] + edge[i + 1]) / 2
+                s0 = max(0, min(ntok - w, int(round(mid - w / 2))))
+                s1 = max(0, min(ntok - w, int(round(ntok - mid - w / 2))))
+                hold.append((far + 32 + (2, 3, 6, 7)[i], s0, w, x, i, 0x000F))
+                hold.append((far + 64 + (2, 3, 6, 7)[i], s1, w, x, i, 0x00F0))
+                hold.append((base + (0, 1, 4, 5)[i], s0, w, x, i, 0x0F00))
+                if i < 3:
+                    hold.append((base + (2, 3, 7)[i], s0, w, x, i, 0xF000))
+            hold.append((me, 0, ntok, RANK_CAP, -1, 0))
+            cap = {}
+            for i, hd in enumerate(hold):
+                cap[2 * i] = hd[3]
+                cap[2 * i + 1] = 8
             elig = []
             for t in range(ntok):
                 d = cores[route[r][t][0]]
-                el = []
-                for i, (k, s, e) in enumerate(hold):
-                    if k != d and s <= t < e and topo.may_write(k, d):
-                        el.append(2 * i + (1 if k // 8 == d // 8 else 0))
-                elig.append(el)
-            owner = match(elig, 8)
-        busy = set()
-        for i, (k, s, e) in enumerate(hold):
-            call = []
-            for on in (0, 1):
-                toks = sorted(owner.get(2 * i + on, []))
-                for t, mk in zip(toks, masks(len(toks), 8 * on)):
+                elig.append([2 * i + (1 if hd[0] // 8 == d // 8 else 0) for i, hd in enumerate(hold)
+                             if hd[0] != d and hd[1] <= t < hd[1] + hd[2] and topo.may_write(hd[0], d)])
+            owner = match(elig, cap)
+        rep = [[], [], [], []]
+        for i, hd in enumerate(hold):
+            k = hd[0]
+            calls = []
+            for toks in chunks(sorted(owner.get(2 * i, []))):
+                calls.append([(t, mk) for t, mk in zip(toks, masks(len(toks), 0))])
+            home = sorted(owner.get(2 * i + 1, []))
+            if home:
+                if not calls:
+                    calls.append([])
+                calls[0] += [(t, mk) for t, mk in zip(home, masks(len(home), 8))]
+            if not calls:
+                continue
+            full = []
+            for call in calls:
+                lst = []
+                for t, mk in call:
                     x = route[r][t][0]
-                    call.append((t, cores[x], pos[r][t], mk))
+                    lst.append((t, cores[x], pos[r][t], mk))
                     plan["arr"][x] += bin(mk).count("1")
-            if call:
-                plan["calls"][k] = [call]
-                busy.add(k)
-        rep = []
-        for i in range(4):
-            for on in (0, 1):
-                dsts = [k for k, j in team if j == i and k in busy and (k // 8 == me // 8) == (on == 1)]
-                if dsts:
-                    rep.append((start[i], w, dsts, 3 << (8 * on + 2 * i)))
-                    for k in dsts:
-                        plan["wait"][k] = 2
-        plan["rep"][me] = rep
+                full.append(lst)
+            plan["calls"][k] = full
+            if k != me:
+                rep[hd[4]].append((hd[1], hd[2], [k], hd[5]))
+                plan["wait"][k] = 4
+        plan["rep"][me] = [x for x in rep if x]
     return plan
 
 
@@ -117,12 +146,13 @@ def rank_program(g, core, T, topo):
     if rank is not None:
         g.sync.dma_start(T.xs[:, :], T.x[:, :]).then_inc(sem.loaded, 16)
         g.wait_ge(sem.loaded, 16)
-        trs = []
-        for s, w, dsts, mk in p["rep"][core]:
-            trs.append(RemoteDMATransfer(dst_ids=[dst_id(d) for d in dsts], dma_engine_mask=mk, remote_sem=sem.rep,
-                                         srcs=[T.xs[:, s:s + w]], dsts=[T.xs[:, s:s + w] for d in dsts]))
-            sent += bin(mk).count("1")
-        g.remote_dma_fused(trs, local_sem=sem.sent)
+        for wave in p["rep"][core]:
+            trs = []
+            for s, w, dsts, mk in wave:
+                trs.append(RemoteDMATransfer(dst_ids=[dst_id(d) for d in dsts], dma_engine_mask=mk, remote_sem=sem.rep,
+                                             srcs=[T.xs[:, s:s + w]], dsts=[T.xs[:, s:s + w] for d in dsts]))
+                sent += bin(mk).count("1")
+            g.remote_dma_fused(trs, local_sem=sem.sent)
     else:
         g.wait_ge(sem.rep, p["wait"][core])
     for call in p["calls"].get(core, []):

@@ -52,6 +52,19 @@ def chunks(toks):
     return out
 
 
+def hops(topo, a, b):
+    n = 0
+    if topo.rack(topo.host(a)) != topo.rack(topo.host(b)):
+        n += 1
+        if topo.chip(a) == topo.chip(b):
+            return n
+    if topo.chip(a) % 2 != topo.chip(b) % 2:
+        n += 1
+        if topo.chip(a) ^ 1 == topo.chip(b) and (n == 2 or topo.host(a) == topo.host(b)):
+            return n
+    return n + 1
+
+
 def build_plan(cores, route, topo):
     n = len(cores)
     ntok = len(route[0])
@@ -104,7 +117,8 @@ def build_plan(cores, route, topo):
         for i, hd in enumerate(hold):
             k = hd[0]
             calls = []
-            for toks in chunks(sorted(owner.get(2 * i, []))):
+            away = sorted((-hops(topo, k, cores[route[r][t][0]]), t) for t in owner.get(2 * i, []))
+            for toks in chunks([t for q, t in away]):
                 calls.append([(t, mk) for t, mk in zip(toks, masks(len(toks), 0))])
             home = sorted(owner.get(2 * i + 1, []))
             if home:

@@ -7,8 +7,11 @@ SCRATCH = {
 SEMAPHORES = ["loaded", "rep", "arr", "sent", "stored"]
 
 PLAN = {}
-CAPS = (12, 10, 6, 5)
-RANK_CAP = 4
+CAPS = (12, 10, 7, 5)
+FIRST = (8, 8, 4, 4)
+RANK_CAP = 6
+TRIES = ([((1, 1, 2, 1), m) for m in (0, 1, 2)] + [((2, 1, 2, 1), m) for m in (0, 1, 2)]
+         + [((2, 2, 2, 2), m) for m in (0, 1, 2)] + [((3, 3, 3, 3), m) for m in range(64)])
 
 
 def match(elig, cap):
@@ -88,9 +91,7 @@ def build_plan(cores, route, topo):
         base = me - me % 8
         far = (h ^ 1) * 128 + c * 8
         owner = None
-        m = -1
-        while owner is None:
-            m += 1
+        for lim, m in TRIES:
             hold = []
             for i, x in enumerate(CAPS):
                 w = min(ntok, -(-ntok * x // tot) + 2 * m)
@@ -105,22 +106,35 @@ def build_plan(cores, route, topo):
             hold.append((me, 0, ntok, RANK_CAP, -1, 0))
             cap = {}
             for i, hd in enumerate(hold):
-                cap[2 * i] = hd[3]
-                cap[2 * i + 1] = 8
+                first = FIRST[hd[4]] if hd[4] >= 0 else hd[3]
+                cap[3 * i] = first
+                cap[3 * i + 1] = 8
+                cap[3 * i + 2] = hd[3] - first
             elig = []
             for t in range(ntok):
                 d = cores[route[r][t][0]]
-                elig.append([2 * i + (1 if hd[0] // 8 == d // 8 else 0) for i, hd in enumerate(hold)
-                             if hd[0] != d and hd[1] <= t < hd[1] + hd[2] and topo.may_write(hd[0], d)])
+                el = []
+                for i, hd in enumerate(hold):
+                    if hd[0] != d and hd[1] <= t < hd[1] + hd[2] and topo.may_write(hd[0], d):
+                        if hd[0] // 8 == d // 8:
+                            el.append(3 * i + 1)
+                        else:
+                            if hd[4] >= 0 and hops(topo, hd[0], d) <= lim[hd[4]]:
+                                el.append(3 * i + 2)
+                            el.append(3 * i)
+                elig.append(el)
             owner = match(elig, cap)
+            if owner is not None:
+                break
         rep = [[], [], [], []]
         for i, hd in enumerate(hold):
             k = hd[0]
             calls = []
-            away = sorted((-hops(topo, k, cores[route[r][t][0]]), t) for t in owner.get(2 * i, []))
+            away = sorted((-hops(topo, k, cores[route[r][t][0]]), t)
+                          for t in owner.get(3 * i, []) + owner.get(3 * i + 2, []))
             for toks in chunks([t for q, t in away]):
                 calls.append([(t, mk) for t, mk in zip(toks, masks(len(toks), 0))])
-            home = sorted(owner.get(2 * i + 1, []))
+            home = sorted(owner.get(3 * i + 1, []))
             if home:
                 if not calls:
                     calls.append([])

from concourse.bass import DstId, RemoteDMATransfer

SCRATCH = {
    "xs": ("sbuf", [128, 128], "float32"),
    "land": ("sbuf", [128, 147], "float32"),
}
SEMAPHORES = ["loaded", "rep", "arr", "sent", "stored"]

PLAN = {}
CAPS = (12, 10, 7, 5)
FIRST = (8, 8, 4, 4)
RANK_CAP = 6
TRIES = ([((1, 1, 2, 1), m) for m in (0, 1, 2)] + [((2, 1, 2, 1), m) for m in (0, 1, 2)]
         + [((2, 2, 2, 2), m) for m in (0, 1, 2)] + [((3, 3, 3, 3), m) for m in range(64)])


def match(elig, cap):
    owner = {}

    def place(t, seen):
        for n in elig[t]:
            if n in seen:
                continue
            seen.add(n)
            lst = owner.setdefault(n, [])
            if len(lst) < cap[n]:
                lst.append(t)
                return True
            for j in range(len(lst)):
                if place(lst[j], seen):
                    lst[j] = t
                    return True
        return False

    for t in range(len(elig)):
        if not place(t, set()):
            return None
    return owner


def masks(n, base):
    k = 8
    while k * n > 8:
        k //= 2
    return [((1 << k) - 1) << (base + i * k) for i in range(n)]


def chunks(toks):
    out = []
    i = 0
    for size in (8, 8, 4, 2, 1):
        if len(toks) - i >= size:
            out.append(toks[i:i + size])
            i += size
    return out


def hops(topo, a, b):
    n = 0
    if topo.rack(topo.host(a)) != topo.rack(topo.host(b)):
        n += 1
        if topo.chip(a) == topo.chip(b):
            return n
    if topo.chip(a) % 2 != topo.chip(b) % 2:
        n += 1
        if topo.chip(a) ^ 1 == topo.chip(b) and (n == 2 or topo.host(a) == topo.host(b)):
            return n
    return n + 1


def build_plan(cores, route, topo):
    n = len(cores)
    ntok = len(route[0])
    fill = [0] * n
    pos = []
    for r in range(n):
        row = []
        for t in range(ntok):
            e = route[r][t][0]
            row.append(fill[e])
            fill[e] += 1
        pos.append(row)
    plan = {"count": fill, "rep": {}, "wait": {}, "calls": {}, "arr": [0] * n}
    tot = sum(CAPS)
    edge = [0]
    for x in CAPS:
        edge.append(edge[-1] + ntok * x / tot)
    for r in range(n):
        me = cores[r]
        h, c = topo.host(me), topo.chip(me)
        base = me - me % 8
        far = (h ^ 1) * 128 + c * 8
        owner = None
        for lim, m in TRIES:
            hold = []
            for i, x in enumerate(CAPS):
                w = min(ntok, -(-ntok * x // tot) + 2 * m)
                mid = (edge[i] + edge[i + 1]) / 2
                s0 = max(0, min(ntok - w, int(round(mid - w / 2))))
                s1 = max(0, min(ntok - w, int(round(ntok - mid - w / 2))))
                hold.append((far + 32 + (2, 3, 6, 7)[i], s0, w, x, i, 0x000F))
                hold.append((far + 64 + (2, 3, 6, 7)[i], s1, w, x, i, 0x00F0))
                hold.append((base + (0, 1, 4, 5)[i], s0, w, x, i, 0x0F00))
                if i < 3:
                    hold.append((base + (2, 3, 7)[i], s0, w, x, i, 0xF000))
            hold.append((me, 0, ntok, RANK_CAP, -1, 0))
            cap = {}
            for i, hd in enumerate(hold):
                first = FIRST[hd[4]] if hd[4] >= 0 else hd[3]
                cap[3 * i] = first
                cap[3 * i + 1] = 8
                cap[3 * i + 2] = hd[3] - first
            elig = []
            for t in range(ntok):
                d = cores[route[r][t][0]]
                el = []
                for i, hd in enumerate(hold):
                    if hd[0] != d and hd[1] <= t < hd[1] + hd[2] and topo.may_write(hd[0], d):
                        if hd[0] // 8 == d // 8:
                            el.append(3 * i + 1)
                        else:
                            if hd[4] >= 0 and hops(topo, hd[0], d) <= lim[hd[4]]:
                                el.append(3 * i + 2)
                            el.append(3 * i)
                elig.append(el)
            owner = match(elig, cap)
            if owner is not None:
                break
        rep = [[], [], [], []]
        for i, hd in enumerate(hold):
            k = hd[0]
            calls = []
            away = sorted((-hops(topo, k, cores[route[r][t][0]]), t)
                          for t in owner.get(3 * i, []) + owner.get(3 * i + 2, []))
            for toks in chunks([t for q, t in away]):
                calls.append([(t, mk) for t, mk in zip(toks, masks(len(toks), 0))])
            home = sorted(owner.get(3 * i + 1, []))
            if home:
                if not calls:
                    calls.append([])
                calls[0] += [(t, mk) for t, mk in zip(home, masks(len(home), 8))]
            if not calls:
                continue
            full = []
            for call in calls:
                lst = []
                for t, mk in call:
                    x = route[r][t][0]
                    lst.append((t, cores[x], pos[r][t], mk))
                    plan["arr"][x] += bin(mk).count("1")
                full.append(lst)
            plan["calls"][k] = full
            if k != me:
                rep[hd[4]].append((hd[1], hd[2], [k], hd[5]))
                plan["wait"][k] = 4
        plan["rep"][me] = [x for x in rep if x]
    return plan


def rank_program(g, core, T, topo):
    if "p" not in PLAN:
        PLAN["p"] = build_plan(T.cores, T.tables["ROUTE"], topo)
    p = PLAN["p"]
    rank = T.rank_of(core)
    if rank is None and core not in p["wait"]:
        return
    sem = T.sem

    def dst_id(d):
        rid, pid = topo.addr(d, core)
        return DstId(rid=rid, pnc=pid)

    sent = 0
    if rank is not None:
        g.sync.dma_start(T.xs[:, :], T.x[:, :]).then_inc(sem.loaded, 16)
        g.wait_ge(sem.loaded, 16)
        for wave in p["rep"][core]:
            trs = []
            for s, w, dsts, mk in wave:
                trs.append(RemoteDMATransfer(dst_ids=[dst_id(d) for d in dsts], dma_engine_mask=mk, remote_sem=sem.rep,
                                             srcs=[T.xs[:, s:s + w]], dsts=[T.xs[:, s:s + w] for d in dsts]))
                sent += bin(mk).count("1")
            g.remote_dma_fused(trs, local_sem=sem.sent)
    else:
        g.wait_ge(sem.rep, p["wait"][core])
    for call in p["calls"].get(core, []):
        trs = []
        for t, d, j, mk in call:
            trs.append(RemoteDMATransfer(dst_ids=[dst_id(d)], dma_engine_mask=mk, remote_sem=sem.arr,
                                         src=T.xs[:, t:t + 1], dst=T.land[:, j:j + 1]))
            sent += bin(mk).count("1")
        g.remote_dma_fused(trs, local_sem=sem.sent)
    if rank is not None:
        cnt = p["count"][rank]
        g.sync.wait_ge(sem.arr, p["arr"][rank])
        g.sync.dma_start(T.y[:, 0:cnt], T.land[:, 0:cnt]).then_inc(sem.stored, 16)
        g.wait_ge(sem.stored, 16)
    g.wait_ge(sem.sent, sent)
